import numpy as np
import ml_dtypes


def mxq(x, axis, fmt="e4m3"):
    dtype, down = {"e4m3": (ml_dtypes.float8_e4m3fn, 7), "e5m2": (ml_dtypes.float8_e5m2, 14)}[fmt]
    v = np.moveaxis(np.asarray(x, np.float32).astype(ml_dtypes.bfloat16).astype(np.float64), axis, -1)
    blocks = v.reshape(v.shape[:-1] + (-1, 32))
    amax = np.abs(blocks).max(-1, keepdims=True)
    byte = np.maximum(np.where(amax > 0, np.frexp(amax)[1] - 1 + 127, 0) - down, 1)
    scale = np.exp2(byte - 127.0)
    codes = (blocks / scale).astype(np.float32).astype(dtype).astype(np.float64)
    return np.moveaxis((codes * scale).reshape(v.shape), -1, axis)


WIDE = False


def mx_kscale(k):
    if not WIDE:
        return np.ones(k)
    levels = np.array([10, -10, 5, -5, 0])
    if k % 512:
        return np.exp2(np.random.permutation(np.resize(levels, k // 32))).repeat(32)
    a = np.empty((k // 512, 16))
    for p in range(k // 512):
        a[p, :8] = np.random.permutation(np.resize(levels, 8))
        for g in range(8):
            far = levels[np.abs(levels - a[p, g]) >= 10]
            a[p, g + 8] = far[np.random.randint(len(far))]
    return np.exp2(a.ravel()).repeat(32)


def f64(x):
    return np.asarray(x).astype(np.float64)


def striped8(idx):
    return np.asarray(idx).reshape(8, -1, 16).transpose(0, 2, 1).reshape(128, -1).astype(np.uint16)


def unstriped8(offs):
    return offs.reshape(8, 16, -1).transpose(0, 2, 1).reshape(8, -1).astype(np.int64)


def pick8(x, idx, run):
    r = np.arange(len(x))
    return x[r[:, None], idx[r % (8 * run) // run]]


E2M1 = np.array([0.0, 0.5, 1.0, 1.5, 2.0, 3.0, 4.0, 6.0, -0.0, -0.5, -1.0, -1.5, -2.0, -3.0, -4.0, -6.0])


def pack_weight(w, fmt):
    k, n = w.shape
    w = f64(np.asarray(w, np.float32).astype(ml_dtypes.bfloat16)).reshape(k // 32, 32, n)
    amax = np.abs(w).max(1)
    if fmt == "e4m3":
        byte = np.frexp(amax)[1] - 1 + 127 - 7
    else:
        mant, ex = np.frexp(amax / 6.0)
        byte = np.where(mant > 0.5, ex, ex - 1) + 127
    byte = np.clip(np.where(amax > 0, byte, 1), 1, 254)
    scaled = (w * np.exp2(127.0 - byte)[:, None, :]).reshape(k, n).astype(np.float32)
    by_word = np.ascontiguousarray(scaled.reshape(k // 512, 128, 4, n).transpose(0, 1, 3, 2))
    if fmt == "e4m3":
        words = by_word.astype(ml_dtypes.float8_e4m3fn).view(np.uint8)
    else:
        c = by_word.astype(ml_dtypes.float4_e2m1fn).view(np.uint8) & 0xF
        words = (c[..., 0::2] | (c[..., 1::2] << 4)).reshape(k // 512, 128, 2 * n)
    return np.ascontiguousarray(words), np.ascontiguousarray(byte.astype(np.uint8).reshape(k // 512, 16, n))


def unpack_weight(words, scales, fmt):
    g, _, n = scales.shape
    words = np.ascontiguousarray(words).reshape(g, 128, n, -1)
    if fmt == "e4m3":
        vals = words.view(ml_dtypes.float8_e4m3fn).astype(np.float64)
    else:
        nib = np.empty((g, 128, n, 4), np.uint8)
        nib[..., 0::2] = words & 0xF
        nib[..., 1::2] = words >> 4
        vals = E2M1[nib]
    vals = vals * np.repeat(np.exp2(scales.astype(np.float64) - 127.0), 8, axis=1)[..., None]
    return vals.transpose(0, 1, 3, 2).reshape(g * 512, n)


def sigmoid(v):
    return 1.0 / (1.0 + np.exp(-v))


def sgn(shape):
    return np.random.uniform(0.5, 2.0, shape) * np.where(np.random.standard_normal(shape) < 0, -1.0, 1.0)


D, T, U, X, I, Q = 512, 1024, 1024, 1024, 512, 128


def setup_inputs():
    n = np.random.standard_normal
    idx = np.stack([np.random.permutation(X)[:I] for _ in range(8)])
    idx2 = np.stack([np.random.permutation(T)[:I] for _ in range(8)])
    idx3 = np.stack([np.random.permutation(T)[:I] for _ in range(8)])
    idx4 = np.stack([np.random.permutation(U)[:I] for _ in range(8)])
    idx5 = np.stack([np.random.permutation(T)[:I] for _ in range(8)])
    idx6 = np.stack([np.random.permutation(U)[:I] for _ in range(8)])
    fd = mx_kscale(D)
    cachep = pack_weight(n((D, T)) / fd[:, None], "e2m1")
    draftp = pack_weight(n((D, U)) / fd[:, None], "e4m3")
    archp = pack_weight(n((D, X)) / fd[:, None], "e2m1")
    return {
        "query": (n((D, Q)) * 1.0 / np.sqrt(D) * fd[:, None]).astype(np.float32),
        "cache_words": cachep[0],
        "cache_scales": cachep[1],
        "draft_words": draftp[0],
        "draft_scales": draftp[1],
        "arch_words": archp[0],
        "arch_scales": archp[1],
        "thr": (np.random.uniform(-2.0, 2.0, (Q, 1))).astype(np.float32),
        "slope": (sgn((Q, 1))).astype(np.float32),
        "offs": striped8(idx),
        "offs2": striped8(idx2),
        "offs3": striped8(idx3),
        "offs4": striped8(idx4),
        "offs5": striped8(idx5),
        "offs6": striped8(idx6),
    }


def reference(query, cache_words, cache_scales, draft_words, draft_scales, arch_words, arch_scales, thr, slope, offs, offs2, offs3, offs4, offs5, offs6):
    idx = unstriped8(offs)
    idx2 = unstriped8(offs2)
    idx3 = unstriped8(offs3)
    idx4 = unstriped8(offs4)
    idx5 = unstriped8(offs5)
    idx6 = unstriped8(offs6)
    cacheu = unpack_weight(cache_words, cache_scales, "e2m1")
    draftu = unpack_weight(draft_words, draft_scales, "e4m3")
    archu = unpack_weight(arch_words, arch_scales, "e2m1")
    queryq = mxq(f64(query), 0, "e4m3")
    a = queryq.T @ cacheu
    b = queryq.T @ draftu
    c0 = queryq.T @ archu
    s1 = sigmoid(pick8(c0, idx, 16) * f64(slope) + f64(thr))
    kp = np.zeros((Q, T))
    kp[np.arange(Q)[:, None], idx2[np.arange(Q) % 128 // 16]] = s1
    ev = a * kp
    aa = a - ev
    f1 = np.zeros((Q, U))
    f1[np.arange(Q)[:, None], idx4[np.arange(Q) % 128 // 16]] = pick8(ev, idx3, 16)
    bb = b + f1
    y = np.maximum(pick8(aa, idx5, 16), pick8(bb, idx6, 16))
    return y

@@ -1,0 +1,145 @@
+from contextlib import ExitStack
+
+import concourse.mybir as mybir
+
+D, T, U, X, I, Q = 512, 1024, 1024, 1024, 512, 128
+FLOPS = 2 * D * Q * (T + U + X)
+
+F32 = mybir.dt.float32
+BF16 = mybir.dt.bfloat16
+I32 = mybir.dt.int32
+U32 = mybir.dt.uint32
+U16 = mybir.dt.uint16
+U8 = mybir.dt.uint8
+FP8X4 = mybir.dt.float8_e4m3fn_x4
+FP4X4 = mybir.dt.float4_e2m1fn_x4
+ALU = mybir.AluOpType
+ACT = mybir.ActivationFunctionType
+
+P = 128
+PACK = 4
+BANK = 512
+HALF = I // 2
+HALF_COLS = HALF // 16
+GATE_N = 256
+
+
+def tile_attend_fadeout_three_kernel(tc, query, cache_words, cache_scales, draft_words, draft_scales,
+                                      arch_words, arch_scales, thr, slope,
+                                      offs, offs2, offs3, offs4, offs5, offs6, out):
+    nc = tc.nc
+    with ExitStack() as ctx:
+        sb = ctx.enter_context(tc.tile_pool(name="sb", bufs=1))
+        ps = ctx.enter_context(tc.psum_pool(name="ps", bufs=1))
+
+        def load_list(src, name):
+            lst = sb.tile([P, I // 16], U16, name=name)
+            nc.sync.dma_start(lst[:], src)
+            return lst
+
+        def load_scale_rows(src, name):
+            rows = sb.tile([4, 4, src.shape[2] // 4], I32, name=name)
+            nc.sync.dma_start(rows[:], src[0].bitcast(I32).rearrange("(quad r) c -> r quad c", r=4))
+            return rows
+
+        def spread_plane(rows, name):
+            plane = sb.tile([P, 4 * rows.shape[2]], U8, name=name, align_bytes=64)
+            nc.vector.memset(plane[:].bitcast(I32), 0)
+            for quad in range(4):
+                nc.vector.tensor_copy(out=plane[32 * quad : 32 * quad + 4, :].bitcast(I32), in_=rows[:, quad, :])
+            return plane
+
+        def load_words(src, name):
+            words = sb.tile([P, src.shape[1]], U8, name=name, align_bytes=64)
+            nc.sync.dma_start(words[:].bitcast(I32), src.bitcast(I32))
+            return words
+
+        arch_rows = load_scale_rows(arch_scales, "arch_rows")
+        q_raw = sb.tile([P, PACK, Q], F32)
+        nc.sync.dma_start(q_raw[:], query.rearrange("(p j) q -> p j q", j=PACK))
+        arch_w = load_words(arch_words[0], "arch_w")
+        list1 = load_list(offs, "list1")
+        slope_t = sb.tile([P, 1], F32)
+        nc.sync.dma_start(slope_t[:], slope)
+        thr_t = sb.tile([P, 1], F32)
+        nc.sync.dma_start(thr_t[:], thr)
+        list2 = load_list(offs2, "list2")
+
+        arch_s = spread_plane(arch_rows, "arch_s")
+        q_bf = sb.tile([P, Q, PACK], BF16, align_bytes=64)
+        q_codes = sb.tile([P, Q], U32, align_bytes=64)
+        q_scales = sb.tile([P, Q], U8, align_bytes=64)
+        halves = [slice(0, Q // 2), slice(Q // 2, Q)]
+        for cols in halves:
+            nc.vector.tensor_copy(out=q_bf[:, cols, :], in_=q_raw[:, :, cols].rearrange("p j q -> p q j"))
+        for cols in halves:
+            nc.vector.quantize_mx(out=q_codes[:, cols].bitcast(FP8X4), scales=q_scales[:, cols],
+                                  in_=q_bf[:, cols, :].rearrange("p q j -> p (q j)"))
+
+        def score(words, bytes_per_col, fmt, plane, start, width, name):
+            acc = ps.tile([Q, width], F32, name=name)
+            nc.tensor.matmul_mx(out=acc[:], lhsT=q_codes[:].bitcast(FP8X4), lhsT_scale=q_scales[:],
+                                rhs=words[:, bytes_per_col * start : bytes_per_col * (start + width)].bitcast(fmt),
+                                rhs_scale=plane[:, start : start + width], start=True, stop=True)
+            return acc
+
+        c0 = sb.tile([Q, X], F32, tag="c0_then_f1")
+        for n in range(X // GATE_N):
+            acc = score(arch_w, 2, FP4X4, arch_s, n * GATE_N, GATE_N, "c0_%d" % n)
+            dst = c0[:, n * GATE_N : (n + 1) * GATE_N]
+            nc.vector.tensor_copy(out=dst, in_=acc[:])
+
+        s1 = sb.tile([Q, I], F32)
+        nc.scalar.activation(s1[:], c0[:].indirect(list1[:]), ACT.Sigmoid, bias=thr_t[:], scale=slope_t[:])
+        kp = sb.tile([Q, T], F32, tag="kp_then_aa")
+        nc.vector.memset(kp[:], 0.0)
+        nc.scalar.activation(kp[:].indirect(list2[:]), s1[:], ACT.Copy)
+
+        cache_rows = load_scale_rows(cache_scales, "cache_rows")
+        draft_rows = load_scale_rows(draft_scales, "draft_rows")
+        cache_w = load_words(cache_words[0], "cache_w")
+        draft_w = load_words(draft_words[0].rearrange("p c r -> p (c r)"), "draft_w")
+        cache_s = spread_plane(cache_rows, "cache_s")
+        draft_s = spread_plane(draft_rows, "draft_s")
+        list3 = load_list(offs3, "list3")
+        list4 = load_list(offs4, "list4")
+        list5 = load_list(offs5, "list5")
+        list6 = load_list(offs6, "list6")
+
+        a = [score(cache_w, 2, FP4X4, cache_s, n * BANK, BANK, "a_%d" % n) for n in range(T // BANK)]
+        b = [score(draft_w, 4, FP8X4, draft_s, n * BANK, BANK, "b_%d" % n) for n in range(U // BANK)]
+
+        ev = sb.tile([Q, T], F32)
+        for n in range(T // BANK):
+            cols = slice(n * BANK, (n + 1) * BANK)
+            nc.vector.tensor_tensor(ev[:, cols], a[n][:], kp[:, cols], ALU.mult)
+
+        f1 = sb.tile([Q, U], F32, tag="c0_then_f1")
+        nc.vector.memset(f1[:], 0.0)
+        moved = sb.tile([Q, I], F32)
+        for h in range(2):
+            slots = slice(h * HALF, (h + 1) * HALF)
+            lcols = slice(h * HALF_COLS, (h + 1) * HALF_COLS)
+            nc.vector.tensor_copy(out=moved[:, slots], in_=ev[:].indirect(list3[:, lcols]))
+            nc.scalar.activation(f1[:].indirect(list4[:, lcols]), moved[:, slots], ACT.Copy)
+
+        aa = sb.tile([Q, T], F32, tag="kp_then_aa")
+        for n in range(T // BANK):
+            cols = slice(n * BANK, (n + 1) * BANK)
+            nc.vector.tensor_tensor(aa[:, cols], a[n][:], ev[:, cols], ALU.subtract)
+        aa_g = sb.tile([Q, I], F32)
+        nc.vector.tensor_copy(out=aa_g[:], in_=aa[:].indirect(list5[:]))
+
+        bb = sb.tile([Q, U], F32)
+        for n in range(U // BANK):
+            cols = slice(n * BANK, (n + 1) * BANK)
+            nc.vector.tensor_tensor(bb[:, cols], b[n][:], f1[:, cols], ALU.add)
+
+        bb_g = sb.tile([Q, I], F32)
+        nc.vector.tensor_copy(out=bb_g[:, 0:HALF], in_=bb[:].indirect(list6[:, 0:HALF_COLS]))
+        nc.scalar.activation(bb_g[:, HALF:I], bb[:].indirect(list6[:, HALF_COLS : 2 * HALF_COLS]), ACT.Copy)
+        res = sb.tile([Q, I], F32)
+        for h in (1, 0):
+            slots = slice(h * HALF, (h + 1) * HALF)
+            nc.vector.tensor_tensor(res[:, slots], aa_g[:, slots], bb_g[:, slots], ALU.max)
+            nc.sync.dma_start(out[:, slots], res[:, slots])

@@ -42,30 +42,34 @@ def tile_attend_fadeout_three_kernel(tc, query, cache_words, cache_scales, draft
             nc.sync.dma_start(rows[:], src[0].bitcast(I32).rearrange("(quad r) c -> r quad c", r=4))
             return rows
 
-        def spread_plane(rows, name):
-            plane = sb.tile([P, 4 * rows.shape[2]], U8, name=name, align_bytes=64)
+        def zeroed_plane(name, tag):
+            plane = sb.tile([P, T], U8, name=name, tag=tag, align_bytes=64)
             nc.vector.memset(plane[:].bitcast(I32), 0)
-            for quad in range(4):
-                nc.vector.tensor_copy(out=plane[32 * quad : 32 * quad + 4, :].bitcast(I32), in_=rows[:, quad, :])
             return plane
 
+        def spread(rows, plane):
+            for quad in range(4):
+                nc.vector.tensor_copy(out=plane[32 * quad : 32 * quad + 4, :].bitcast(I32), in_=rows[:, quad, :])
+
         def load_words(src, name):
-            words = sb.tile([P, src.shape[1]], U8, name=name, align_bytes=64)
+            words = sb.tile([P, src.shape[1]], U8, name=name, tag=name, align_bytes=64)
             nc.sync.dma_start(words[:].bitcast(I32), src.bitcast(I32))
             return words
 
-        arch_rows = load_scale_rows(arch_scales, "arch_rows")
         q_raw = sb.tile([P, PACK, Q], F32)
         nc.sync.dma_start(q_raw[:], query.rearrange("(p j) q -> p j q", j=PACK))
+        fp4_s = zeroed_plane("fp4_s", "fp4_s")
+        for quad in range(4):
+            nc.sync.dma_start(fp4_s[32 * quad : 32 * quad + 4, :].bitcast(I32),
+                              arch_scales[0, 4 * quad : 4 * quad + 4, :].bitcast(I32))
         arch_w = load_words(arch_words[0], "arch_w")
         list1 = load_list(offs, "list1")
         slope_t = sb.tile([P, 1], F32)
         nc.sync.dma_start(slope_t[:], slope)
         thr_t = sb.tile([P, 1], F32)
-        nc.sync.dma_start(thr_t[:], thr)
+        nc.gpsimd.dma_start(thr_t[:], thr)
         list2 = load_list(offs2, "list2")
 
-        arch_s = spread_plane(arch_rows, "arch_s")
         q_bf = sb.tile([P, Q, PACK], BF16, align_bytes=64)
         q_codes = sb.tile([P, Q], U32, align_bytes=64)
         q_scales = sb.tile([P, Q], U8, align_bytes=64)
@@ -85,28 +89,29 @@ def tile_attend_fadeout_three_kernel(tc, query, cache_words, cache_scales, draft
 
         c0 = sb.tile([Q, X], F32, tag="c0_then_f1")
         for n in range(X // GATE_N):
-            acc = score(arch_w, 2, FP4X4, arch_s, n * GATE_N, GATE_N, "c0_%d" % n)
+            acc = score(arch_w, 2, FP4X4, fp4_s, n * GATE_N, GATE_N, "c0_%d" % n)
             dst = c0[:, n * GATE_N : (n + 1) * GATE_N]
             nc.vector.tensor_copy(out=dst, in_=acc[:])
 
         s1 = sb.tile([Q, I], F32)
         nc.scalar.activation(s1[:], c0[:].indirect(list1[:]), ACT.Sigmoid, bias=thr_t[:], scale=slope_t[:])
-        kp = sb.tile([Q, T], F32, tag="kp_then_aa")
+        kp = sb.tile([Q, T], F32)
         nc.vector.memset(kp[:], 0.0)
         nc.scalar.activation(kp[:].indirect(list2[:]), s1[:], ACT.Copy)
 
         cache_rows = load_scale_rows(cache_scales, "cache_rows")
-        draft_rows = load_scale_rows(draft_scales, "draft_rows")
         cache_w = load_words(cache_words[0], "cache_w")
+        draft_rows = load_scale_rows(draft_scales, "draft_rows")
         draft_w = load_words(draft_words[0].rearrange("p c r -> p (c r)"), "draft_w")
-        cache_s = spread_plane(cache_rows, "cache_s")
-        draft_s = spread_plane(draft_rows, "draft_s")
+        spread(cache_rows, fp4_s)
+        draft_s = zeroed_plane("draft_s", "arch_w")
+        spread(draft_rows, draft_s)
         list3 = load_list(offs3, "list3")
         list4 = load_list(offs4, "list4")
         list5 = load_list(offs5, "list5")
         list6 = load_list(offs6, "list6")
 
-        a = [score(cache_w, 2, FP4X4, cache_s, n * BANK, BANK, "a_%d" % n) for n in range(T // BANK)]
+        a = [score(cache_w, 2, FP4X4, fp4_s, n * BANK, BANK, "a_%d" % n) for n in range(T // BANK)]
         b = [score(draft_w, 4, FP8X4, draft_s, n * BANK, BANK, "b_%d" % n) for n in range(U // BANK)]
 
         ev = sb.tile([Q, T], F32)
@@ -123,14 +128,14 @@ def tile_attend_fadeout_three_kernel(tc, query, cache_words, cache_scales, draft
             nc.vector.tensor_copy(out=moved[:, slots], in_=ev[:].indirect(list3[:, lcols]))
             nc.scalar.activation(f1[:].indirect(list4[:, lcols]), moved[:, slots], ACT.Copy)
 
-        aa = sb.tile([Q, T], F32, tag="kp_then_aa")
+        aa = ev
         for n in range(T // BANK):
             cols = slice(n * BANK, (n + 1) * BANK)
             nc.vector.tensor_tensor(aa[:, cols], a[n][:], ev[:, cols], ALU.subtract)
         aa_g = sb.tile([Q, I], F32)
         nc.vector.tensor_copy(out=aa_g[:], in_=aa[:].indirect(list5[:]))
 
-        bb = sb.tile([Q, U], F32)
+        bb = aa
         for n in range(U // BANK):
             cols = slice(n * BANK, (n + 1) * BANK)
             nc.vector.tensor_tensor(bb[:, cols], b[n][:], f1[:, cols], ALU.add)

@@ -22,6 +22,7 @@ BANK = 512
 HALF = I // 2
 HALF_COLS = HALF // 16
 GATE_N = 256
+SPLIT = 736
 
 
 def tile_attend_fadeout_three_kernel(tc, query, cache_words, cache_scales, draft_words, draft_scales,
@@ -114,37 +115,43 @@ def tile_attend_fadeout_three_kernel(tc, query, cache_words, cache_scales, draft
         a = [score(cache_w, 2, FP4X4, fp4_s, n * BANK, BANK, "a_%d" % n) for n in range(T // BANK)]
         b = [score(draft_w, 4, FP8X4, draft_s, n * BANK, BANK, "b_%d" % n) for n in range(U // BANK)]
 
+        def elementwise(dst, banks, tail, other, op):
+            for n, bank in enumerate(banks):
+                stop = min(BANK, SPLIT - n * BANK)
+                cols = slice(n * BANK, n * BANK + stop)
+                nc.vector.tensor_tensor(dst[:, cols], bank[:, 0:stop], other[:, cols], op)
+            nc.gpsimd.tensor_tensor(dst[:, SPLIT:T], tail[:], other[:, SPLIT:T], op)
+
+        a_tail = sb.tile([Q, T - SPLIT], F32)
+        nc.vector.tensor_copy(out=a_tail[:], in_=a[1][:, SPLIT - BANK : BANK])
+        b_tail = sb.tile([Q, U - SPLIT], F32)
+        nc.vector.tensor_copy(out=b_tail[:], in_=b[1][:, SPLIT - BANK : BANK])
+
+        def gather_halves(dst, window, lst):
+            nc.vector.tensor_copy(out=dst[:, 0:HALF], in_=window[:].indirect(lst[:, 0:HALF_COLS]))
+            nc.scalar.activation(dst[:, HALF:I], window[:].indirect(lst[:, HALF_COLS : 2 * HALF_COLS]), ACT.Copy)
+
         ev = sb.tile([Q, T], F32)
-        for n in range(T // BANK):
-            cols = slice(n * BANK, (n + 1) * BANK)
-            nc.vector.tensor_tensor(ev[:, cols], a[n][:], kp[:, cols], ALU.mult)
+        elementwise(ev, a, a_tail, kp, ALU.mult)
 
         f1 = sb.tile([Q, U], F32, tag="c0_then_f1")
         nc.vector.memset(f1[:], 0.0)
         moved = sb.tile([Q, I], F32)
-        for h in range(2):
-            slots = slice(h * HALF, (h + 1) * HALF)
-            lcols = slice(h * HALF_COLS, (h + 1) * HALF_COLS)
-            nc.vector.tensor_copy(out=moved[:, slots], in_=ev[:].indirect(list3[:, lcols]))
-            nc.scalar.activation(f1[:].indirect(list4[:, lcols]), moved[:, slots], ACT.Copy)
+        gather_halves(moved, ev, list3)
+        nc.scalar.activation(f1[:].indirect(list4[:]), moved[:], ACT.Copy)
 
         aa = ev
-        for n in range(T // BANK):
-            cols = slice(n * BANK, (n + 1) * BANK)
-            nc.vector.tensor_tensor(aa[:, cols], a[n][:], ev[:, cols], ALU.subtract)
+        elementwise(aa, a, a_tail, ev, ALU.subtract)
         aa_g = sb.tile([Q, I], F32)
         nc.vector.tensor_copy(out=aa_g[:], in_=aa[:].indirect(list5[:]))
 
         bb = aa
-        for n in range(U // BANK):
-            cols = slice(n * BANK, (n + 1) * BANK)
-            nc.vector.tensor_tensor(bb[:, cols], b[n][:], f1[:, cols], ALU.add)
+        elementwise(bb, b, b_tail, f1, ALU.add)
 
         bb_g = sb.tile([Q, I], F32)
-        nc.vector.tensor_copy(out=bb_g[:, 0:HALF], in_=bb[:].indirect(list6[:, 0:HALF_COLS]))
-        nc.scalar.activation(bb_g[:, HALF:I], bb[:].indirect(list6[:, HALF_COLS : 2 * HALF_COLS]), ACT.Copy)
+        gather_halves(bb_g, bb, list6)
         res = sb.tile([Q, I], F32)
-        for h in (1, 0):
+        for h in range(2):
             slots = slice(h * HALF, (h + 1) * HALF)
             nc.vector.tensor_tensor(res[:, slots], aa_g[:, slots], bb_g[:, slots], ALU.max)
             nc.sync.dma_start(out[:, slots], res[:, slots])

@@ -22,7 +22,7 @@ BANK = 512
 HALF = I // 2
 HALF_COLS = HALF // 16
 GATE_N = 256
-SPLIT = 736
+SPLIT = 672
 
 
 def tile_attend_fadeout_three_kernel(tc, query, cache_words, cache_scales, draft_words, draft_scales,
@@ -50,7 +50,7 @@ def tile_attend_fadeout_three_kernel(tc, query, cache_words, cache_scales, draft
 
         def spread(rows, plane):
             for quad in range(4):
-                nc.vector.tensor_copy(out=plane[32 * quad : 32 * quad + 4, :].bitcast(I32), in_=rows[:, quad, :])
+                nc.vector.tensor_copy(out=plane[32 * quad : 32 * quad + 4, 0:T].bitcast(I32), in_=rows[:, quad, :])
 
         def load_words(src, name):
             words = sb.tile([P, src.shape[1]], U8, name=name, tag=name, align_bytes=64)
@@ -59,16 +59,19 @@ def tile_attend_fadeout_three_kernel(tc, query, cache_words, cache_scales, draft
 
         q_raw = sb.tile([P, PACK, Q], F32)
         nc.sync.dma_start(q_raw[:], query.rearrange("(p j) q -> p j q", j=PACK))
-        fp4_s = zeroed_plane("fp4_s", "fp4_s")
-        for quad in range(4):
-            nc.sync.dma_start(fp4_s[32 * quad : 32 * quad + 4, :].bitcast(I32),
-                              arch_scales[0, 4 * quad : 4 * quad + 4, :].bitcast(I32))
+        fp4_s = sb.tile([P, 2 * X], U8, align_bytes=64)
+        nc.vector.memset(fp4_s[:, 0:X].bitcast(I32), 0)
+        arch_rows = arch_scales[0].bitcast(I32)
+        nc.sync.dma_start(fp4_s[0:4, :].bitcast(I32).rearrange("r (quad c) -> r quad c", quad=2),
+                          arch_rows[0:8, :].rearrange("(quad r) c -> r quad c", r=4))
+        for quad in (2, 3):
+            nc.sync.dma_start(fp4_s[32 * quad : 32 * quad + 4, 0:X].bitcast(I32), arch_rows[4 * quad : 4 * quad + 4, :])
         arch_w = load_words(arch_words[0], "arch_w")
-        list1 = load_list(offs, "list1")
         slope_t = sb.tile([P, 1], F32)
         nc.sync.dma_start(slope_t[:], slope)
         thr_t = sb.tile([P, 1], F32)
-        nc.gpsimd.dma_start(thr_t[:], thr)
+        nc.sync.dma_start(thr_t[:], thr)
+        list1 = load_list(offs, "list1")
         list2 = load_list(offs2, "list2")
 
         q_bf = sb.tile([P, Q, PACK], BF16, align_bytes=64)
@@ -76,10 +79,13 @@ def tile_attend_fadeout_three_kernel(tc, query, cache_words, cache_scales, draft
         q_scales = sb.tile([P, Q], U8, align_bytes=64)
         halves = [slice(0, Q // 2), slice(Q // 2, Q)]
         for cols in halves:
-            nc.vector.tensor_copy(out=q_bf[:, cols, :], in_=q_raw[:, :, cols].rearrange("p j q -> p q j"))
+            nc.vector.tensor_copy(out=q_bf[:, cols, :].rearrange("p (c i) j -> p c j i", i=4),
+                                  in_=q_raw[:, :, cols].rearrange("p j (c i) -> p c j i", i=4))
         for cols in halves:
             nc.vector.quantize_mx(out=q_codes[:, cols].bitcast(FP8X4), scales=q_scales[:, cols],
                                   in_=q_bf[:, cols, :].rearrange("p q j -> p (q j)"))
+
+        nc.vector.tensor_copy(out=fp4_s[32:36, 0:X].bitcast(I32), in_=fp4_s[0:4, X : 2 * X].bitcast(I32))
 
         def score(words, bytes_per_col, fmt, plane, start, width, name):
             acc = ps.tile([Q, width], F32, name=name)
@@ -122,10 +128,8 @@ def tile_attend_fadeout_three_kernel(tc, query, cache_words, cache_scales, draft
                 nc.vector.tensor_tensor(dst[:, cols], bank[:, 0:stop], other[:, cols], op)
             nc.gpsimd.tensor_tensor(dst[:, SPLIT:T], tail[:], other[:, SPLIT:T], op)
 
-        a_tail = sb.tile([Q, T - SPLIT], F32)
+        a_tail = sb.tile([Q, T - SPLIT], F32, tag="tail")
         nc.vector.tensor_copy(out=a_tail[:], in_=a[1][:, SPLIT - BANK : BANK])
-        b_tail = sb.tile([Q, U - SPLIT], F32)
-        nc.vector.tensor_copy(out=b_tail[:], in_=b[1][:, SPLIT - BANK : BANK])
 
         def gather_halves(dst, window, lst):
             nc.vector.tensor_copy(out=dst[:, 0:HALF], in_=window[:].indirect(lst[:, 0:HALF_COLS]))
@@ -142,6 +146,8 @@ def tile_attend_fadeout_three_kernel(tc, query, cache_words, cache_scales, draft
 
         aa = ev
         elementwise(aa, a, a_tail, ev, ALU.subtract)
+        b_tail = sb.tile([Q, U - SPLIT], F32, tag="tail")
+        nc.vector.tensor_copy(out=b_tail[:], in_=b[1][:, SPLIT - BANK : BANK])
         aa_g = sb.tile([Q, I], F32)
         nc.vector.tensor_copy(out=aa_g[:], in_=aa[:].indirect(list5[:]))
 

from contextlib import ExitStack

import concourse.mybir as mybir

D, T, U, X, I, Q = 512, 1024, 1024, 1024, 512, 128
FLOPS = 2 * D * Q * (T + U + X)

F32 = mybir.dt.float32
BF16 = mybir.dt.bfloat16
I32 = mybir.dt.int32
U32 = mybir.dt.uint32
U16 = mybir.dt.uint16
U8 = mybir.dt.uint8
FP8X4 = mybir.dt.float8_e4m3fn_x4
FP4X4 = mybir.dt.float4_e2m1fn_x4
ALU = mybir.AluOpType
ACT = mybir.ActivationFunctionType

P = 128
PACK = 4
BANK = 512
HALF = I // 2
HALF_COLS = HALF // 16
GATE_N = 256
SPLIT = 672


def tile_attend_fadeout_three_kernel(tc, query, cache_words, cache_scales, draft_words, draft_scales,
                                      arch_words, arch_scales, thr, slope,
                                      offs, offs2, offs3, offs4, offs5, offs6, out):
    nc = tc.nc
    with ExitStack() as ctx:
        sb = ctx.enter_context(tc.tile_pool(name="sb", bufs=1))
        ps = ctx.enter_context(tc.psum_pool(name="ps", bufs=1))

        def load_list(src, name):
            lst = sb.tile([P, I // 16], U16, name=name)
            nc.sync.dma_start(lst[:], src)
            return lst

        def load_scale_rows(src, name):
            rows = sb.tile([4, 4, src.shape[2] // 4], I32, name=name)
            nc.sync.dma_start(rows[:], src[0].bitcast(I32).rearrange("(quad r) c -> r quad c", r=4))
            return rows

        def zeroed_plane(name, tag):
            plane = sb.tile([P, T], U8, name=name, tag=tag, align_bytes=64)
            nc.vector.memset(plane[:].bitcast(I32), 0)
            return plane

        def spread(rows, plane):
            for quad in range(4):
                nc.vector.tensor_copy(out=plane[32 * quad : 32 * quad + 4, 0:T].bitcast(I32), in_=rows[:, quad, :])

        def load_words(src, name):
            words = sb.tile([P, src.shape[1]], U8, name=name, tag=name, align_bytes=64)
            nc.sync.dma_start(words[:].bitcast(I32), src.bitcast(I32))
            return words

        q_raw = sb.tile([P, PACK, Q], F32)
        nc.sync.dma_start(q_raw[:], query.rearrange("(p j) q -> p j q", j=PACK))
        fp4_s = sb.tile([P, 2 * X], U8, align_bytes=64)
        nc.vector.memset(fp4_s[:, 0:X].bitcast(I32), 0)
        arch_rows = arch_scales[0].bitcast(I32)
        nc.sync.dma_start(fp4_s[0:4, :].bitcast(I32).rearrange("r (quad c) -> r quad c", quad=2),
                          arch_rows[0:8, :].rearrange("(quad r) c -> r quad c", r=4))
        for quad in (2, 3):
            nc.sync.dma_start(fp4_s[32 * quad : 32 * quad + 4, 0:X].bitcast(I32), arch_rows[4 * quad : 4 * quad + 4, :])
        arch_w = load_words(arch_words[0], "arch_w")
        slope_t = sb.tile([P, 1], F32)
        nc.sync.dma_start(slope_t[:], slope)
        thr_t = sb.tile([P, 1], F32)
        nc.sync.dma_start(thr_t[:], thr)
        list1 = load_list(offs, "list1")
        list2 = load_list(offs2, "list2")

        q_bf = sb.tile([P, Q, PACK], BF16, align_bytes=64)
        q_codes = sb.tile([P, Q], U32, align_bytes=64)
        q_scales = sb.tile([P, Q], U8, align_bytes=64)
        halves = [slice(0, Q // 2), slice(Q // 2, Q)]
        for cols in halves:
            nc.vector.tensor_copy(out=q_bf[:, cols, :].rearrange("p (c i) j -> p c j i", i=4),
                                  in_=q_raw[:, :, cols].rearrange("p j (c i) -> p c j i", i=4))
        for cols in halves:
            nc.vector.quantize_mx(out=q_codes[:, cols].bitcast(FP8X4), scales=q_scales[:, cols],
                                  in_=q_bf[:, cols, :].rearrange("p q j -> p (q j)"))

        nc.vector.tensor_copy(out=fp4_s[32:36, 0:X].bitcast(I32), in_=fp4_s[0:4, X : 2 * X].bitcast(I32))

        def score(words, bytes_per_col, fmt, plane, start, width, name):
            acc = ps.tile([Q, width], F32, name=name)
            nc.tensor.matmul_mx(out=acc[:], lhsT=q_codes[:].bitcast(FP8X4), lhsT_scale=q_scales[:],
                                rhs=words[:, bytes_per_col * start : bytes_per_col * (start + width)].bitcast(fmt),
                                rhs_scale=plane[:, start : start + width], start=True, stop=True)
            return acc

        c0 = sb.tile([Q, X], F32, tag="c0_then_f1")
        for n in range(X // GATE_N):
            acc = score(arch_w, 2, FP4X4, fp4_s, n * GATE_N, GATE_N, "c0_%d" % n)
            dst = c0[:, n * GATE_N : (n + 1) * GATE_N]
            nc.vector.tensor_copy(out=dst, in_=acc[:])

        s1 = sb.tile([Q, I], F32)
        nc.scalar.activation(s1[:], c0[:].indirect(list1[:]), ACT.Sigmoid, bias=thr_t[:], scale=slope_t[:])
        kp = sb.tile([Q, T], F32)
        nc.vector.memset(kp[:], 0.0)
        nc.scalar.activation(kp[:].indirect(list2[:]), s1[:], ACT.Copy)

        cache_rows = load_scale_rows(cache_scales, "cache_rows")
        cache_w = load_words(cache_words[0], "cache_w")
        draft_rows = load_scale_rows(draft_scales, "draft_rows")
        draft_w = load_words(draft_words[0].rearrange("p c r -> p (c r)"), "draft_w")
        spread(cache_rows, fp4_s)
        draft_s = zeroed_plane("draft_s", "arch_w")
        spread(draft_rows, draft_s)
        list3 = load_list(offs3, "list3")
        list4 = load_list(offs4, "list4")
        list5 = load_list(offs5, "list5")
        list6 = load_list(offs6, "list6")

        a = [score(cache_w, 2, FP4X4, fp4_s, n * BANK, BANK, "a_%d" % n) for n in range(T // BANK)]
        b = [score(draft_w, 4, FP8X4, draft_s, n * BANK, BANK, "b_%d" % n) for n in range(U // BANK)]

        def elementwise(dst, banks, tail, other, op):
            for n, bank in enumerate(banks):
                stop = min(BANK, SPLIT - n * BANK)
                cols = slice(n * BANK, n * BANK + stop)
                nc.vector.tensor_tensor(dst[:, cols], bank[:, 0:stop], other[:, cols], op)
            nc.gpsimd.tensor_tensor(dst[:, SPLIT:T], tail[:], other[:, SPLIT:T], op)

        a_tail = sb.tile([Q, T - SPLIT], F32, tag="tail")
        nc.vector.tensor_copy(out=a_tail[:], in_=a[1][:, SPLIT - BANK : BANK])

        def gather_halves(dst, window, lst):
            nc.vector.tensor_copy(out=dst[:, 0:HALF], in_=window[:].indirect(lst[:, 0:HALF_COLS]))
            nc.scalar.activation(dst[:, HALF:I], window[:].indirect(lst[:, HALF_COLS : 2 * HALF_COLS]), ACT.Copy)

        ev = sb.tile([Q, T], F32)
        elementwise(ev, a, a_tail, kp, ALU.mult)

        f1 = sb.tile([Q, U], F32, tag="c0_then_f1")
        nc.vector.memset(f1[:], 0.0)
        moved = sb.tile([Q, I], F32)
        gather_halves(moved, ev, list3)
        nc.scalar.activation(f1[:].indirect(list4[:]), moved[:], ACT.Copy)

        aa = ev
        elementwise(aa, a, a_tail, ev, ALU.subtract)
        b_tail = sb.tile([Q, U - SPLIT], F32, tag="tail")
        nc.vector.tensor_copy(out=b_tail[:], in_=b[1][:, SPLIT - BANK : BANK])
        aa_g = sb.tile([Q, I], F32)
        nc.vector.tensor_copy(out=aa_g[:], in_=aa[:].indirect(list5[:]))

        bb = aa
        elementwise(bb, b, b_tail, f1, ALU.add)

        bb_g = sb.tile([Q, I], F32)
        gather_halves(bb_g, bb, list6)
        res = sb.tile([Q, I], F32)
        for h in range(2):
            slots = slice(h * HALF, (h + 1) * HALF)
            nc.vector.tensor_tensor(res[:, slots], aa_g[:, slots], bb_g[:, slots], ALU.max)
            nc.sync.dma_start(out[:, slots], res[:, slots])
